import numpy as np
import ml_dtypes


def mxq(x, axis, fmt="e4m3"):
    dtype, down = {"e4m3": (ml_dtypes.float8_e4m3fn, 7), "e5m2": (ml_dtypes.float8_e5m2, 14)}[fmt]
    v = np.moveaxis(np.asarray(x, np.float32).astype(ml_dtypes.bfloat16).astype(np.float64), axis, -1)
    blocks = v.reshape(v.shape[:-1] + (-1, 32))
    amax = np.abs(blocks).max(-1, keepdims=True)
    byte = np.maximum(np.where(amax > 0, np.frexp(amax)[1] - 1 + 127, 0) - down, 1)
    scale = np.exp2(byte - 127.0)
    codes = (blocks / scale).astype(np.float32).astype(dtype).astype(np.float64)
    return np.moveaxis((codes * scale).reshape(v.shape), -1, axis)


WIDE = False


def mx_kscale(k):
    if not WIDE:
        return np.ones(k)
    levels = np.array([10, -10, 5, -5, 0])
    if k % 512:
        return np.exp2(np.random.permutation(np.resize(levels, k // 32))).repeat(32)
    a = np.empty((k // 512, 16))
    for p in range(k // 512):
        a[p, :8] = np.random.permutation(np.resize(levels, 8))
        for g in range(8):
            far = levels[np.abs(levels - a[p, g]) >= 10]
            a[p, g + 8] = far[np.random.randint(len(far))]
    return np.exp2(a.ravel()).repeat(32)


BF16 = ml_dtypes.bfloat16


def bf(x):
    return np.asarray(x, np.float32).astype(BF16)


def f64(x):
    return np.asarray(x).astype(np.float64)


B, K, D, H, C = 768, 4, 512, 1024, 512


def logsumexp(v, axis):
    m = np.max(v, axis=axis, keepdims=True)
    return m + np.log(np.sum(np.exp(v - m), axis=axis, keepdims=True))


def draw0():
    s, t = mx_kscale(D), mx_kscale(H)
    return {
        "x": bf(np.random.standard_normal((B, D)) * s),
        "r1": bf(1.0 + 0.5 * np.random.standard_normal((K, D))),
        "w1": bf(np.random.standard_normal((D, H)) / np.sqrt(D) / s[:, None]),
        "b1": bf(np.random.standard_normal((K, H)) * 0.3),
        "r2": bf(np.random.standard_normal((K, H)) * t),
        "w2": bf(np.random.standard_normal((H, C)) * 1.5 / np.sqrt(H) / t[:, None]),
    }


def core(x, r1, w1, b1, r2, w2):
    members = r1.shape[0]
    classes = w2.shape[1]
    xr = f64(x)[None, :, :] * f64(r1)[:, None, :]
    a = mxq(xr, 2, "e4m3") @ mxq(f64(w1), 0, "e4m3")
    h = np.maximum(a + f64(b1)[:, None, :], 0.0)
    hr = h * f64(r2)[:, None, :]
    logits = mxq(hr, 2, "e4m3") @ mxq(f64(w2), 0, "e4m3")
    lp = logits - logsumexp(logits, 2)
    mixed = np.squeeze(logsumexp(lp, 0), axis=0)
    return mixed - np.log(members) + np.log(classes)


def e4m3fn_bytes(y):
    return np.clip(np.asarray(y, np.float64), -448.0, 448.0).astype(np.float32).astype(ml_dtypes.float8_e4m3fn).view(np.uint8)


def e4m3fn_values(b):
    return np.asarray(b, np.uint8).view(ml_dtypes.float8_e4m3fn).astype(np.float64)


def setup_inputs():
    d = draw0()
    x0 = np.asarray(d['w2']).astype(np.float64)
    s = (np.max(np.abs(x0), axis=(1,), keepdims=True) / 448.0).astype(np.float32)
    out = {}
    for k, v in d.items():
        if k == 'w2':
            out['w2_bytes'] = e4m3fn_bytes(x0 / s.astype(np.float64))
            out['w2_scale'] = s
        else:
            out[k] = v
    return out


def reference(x, r1, w1, b1, r2, w2_bytes, w2_scale):
    return core(x, r1, w1, b1, r2, e4m3fn_values(w2_bytes) * w2_scale.astype(np.float64))

@@ -1,0 +1,353 @@
+from contextlib import ExitStack
+
+import concourse.mybir as mybir
+from concourse.masks import make_identity
+
+B, K, D, H, C = 768, 4, 512, 1024, 512
+FLOPS = 2 * K * B * (D * H + H * C)
+
+F32 = mybir.dt.float32
+BF16 = mybir.dt.bfloat16
+U32 = mybir.dt.uint32
+U8 = mybir.dt.uint8
+FP8 = mybir.dt.float8_e4m3fn
+FP8X4 = mybir.dt.float8_e4m3fn_x4
+ALU = mybir.AluOpType
+ACT = mybir.ActivationFunctionType
+
+P = 128
+T = 4
+G = H // (P * T)
+NT = B // P
+CH = 2
+N = CH * P
+NCH = NT // CH
+NH = NCH * K * G
+
+
+def tile_tabmbatchensemblelogmeanprob_kernel(tc, x, r1, w1, b1, r2, w2_bytes, w2_scale, out):
+    nc = tc.nc
+    with ExitStack() as ctx:
+        keep = ctx.enter_context(tc.tile_pool(name="keep", bufs=1))
+        work = ctx.enter_context(tc.tile_pool(name="work", bufs=3))
+        two = ctx.enter_context(tc.tile_pool(name="two", bufs=2))
+        ps_a = ctx.enter_context(tc.psum_pool(name="ps_a", bufs=3))
+        ps_l = ctx.enter_context(tc.psum_pool(name="ps_l", bufs=1))
+        ctx.enter_context(tc.manual_schedule())
+
+        vec = keep.tile([P, T * P], BF16, name="vec", align_bytes=64)
+        nc.vector.memset(vec[:], 0.0)
+        ident = keep.tile([P, P], F32, name="ident", align_bytes=64)
+        make_identity(nc, ident[:])
+        one = keep.tile([P, 1], F32, name="one")
+        nc.gpsimd.memset(one[:], 0.0)
+        dummy = keep.tile([P, 1], F32, name="dummy")
+        nc.scalar.activation(out=dummy[:], in_=one[:], func=ACT.Exp)
+
+        xv = x.rearrange("(p i) d -> p i d", i=NT)
+        ov = out.rearrange("(p i) c -> p i c", i=NT)
+        xraw = [keep.tile([P, CH, D], BF16, name="xraw%d" % c, align_bytes=64) for c in range(NCH)]
+        w1raw = [keep.tile([P, T, P * T], BF16, name="w1raw%d" % g, align_bytes=64) for g in range(G)]
+        w1v = w1.rearrange("(p j) h -> p j h", j=T)
+        nc.sync.dma_start(out=xraw[0][:], in_=xv[:, 0:CH, :])
+        nc.sync.dma_start(out=w1raw[0][:], in_=w1v[:, :, 0:P * T])
+        nc.sync.dma_start(out=vec[16:20, :], in_=r1)
+        nc.sync.dma_start(out=vec[0:8, :], in_=r2.rearrange("k (g c) -> (k g) c", g=G))
+        nc.sync.dma_start(out=vec[8:16, :], in_=b1.rearrange("k (g c) -> (k g) c", g=G))
+        nc.sync.dma_start(out=w1raw[1][:], in_=w1v[:, :, P * T:2 * P * T])
+        for c in range(1, NCH):
+            nc.sync.dma_start(out=xraw[c][:], in_=xv[:, c * CH:(c + 1) * CH, :])
+        w2raw = keep.tile([P, G, T, C], U8, name="w2raw", align_bytes=64)
+        nc.sync.dma_start(out=w2raw[:], in_=w2_bytes.rearrange("(g p t) n -> p g t n", p=P, t=T))
+        w2s = keep.tile([P, G, T], F32, name="w2s")
+        nc.sync.dma_start(out=w2s[:], in_=w2_scale.rearrange("(g p t) o -> p g (t o)", p=P, t=T))
+
+        xT = [keep.tile([P, N, T], BF16, name="xT%d" % c, align_bytes=64) for c in range(NCH)]
+
+        def turn_x(c):
+            bank = ps_a.tile([P, CH, 2, P], F32, name="xbank", tag="a")
+            for i in range(CH):
+                words = xraw[c][:, i, :].bitcast(F32)
+                for u in range(2):
+                    nc.tensor.transpose(bank[:, i, u, :], words[:, u:2 * P:2], ident[:])
+            xw = xT[c][:].rearrange("p n t -> p (n t)").bitcast(F32)
+            nc.scalar.copy(out=xw.rearrange("p (i r u) -> p i r u", i=CH, u=2), in_=bank[:].rearrange("p i u r -> p i r u"))
+
+        turn_x(0)
+        vbank = ps_a.tile([P, 2, P], F32, name="vbank", tag="a")
+        vwords = vec[:].bitcast(F32)
+        for u in range(2):
+            nc.tensor.transpose(vbank[:, u, :], vwords[:, u:2 * P:2], ident[:])
+        NV = 2 * K * G + K
+        vt = keep.tile([P, NV, T], BF16, name="vt", align_bytes=64)
+        vtw = vt[:].rearrange("p n t -> p (n t)").bitcast(F32)
+
+        w1c = [keep.tile([P, P * T], U32, name="w1c%d" % g, align_bytes=64) for g in range(G)]
+        w1s = [keep.tile([P, P * T], U8, name="w1s%d" % g, align_bytes=64) for g in range(G)]
+        w1i = [keep.tile([P, P * T, T], BF16, name="w1i%d" % g, align_bytes=64) for g in range(G)]
+
+        def w1_inter(g, copy):
+            for t in range(0, T, 2):
+                copy(out=w1i[g][:, t * P:(t + 2) * P, :].rearrange("p (t m) j -> p t m j", t=2),
+                     in_=w1raw[g][:].rearrange("p j (m t) -> p t m j", t=T)[:, t:t + 2])
+
+        def w1_quant(g):
+            nc.vector.quantize_mx(out=w1c[g][:].bitcast(FP8X4), scales=w1s[g][:], in_=w1i[g][:].rearrange("p n j -> p (n j)"))
+
+        nc.vector.tensor_copy(out=vtw.rearrange("p (n u) -> p n u", u=2), in_=vbank[:, :, 0:NV].rearrange("p u n -> p n u"))
+        r2t = vt[:, 0:K * G, :].rearrange("p n t -> p (n t)")
+        b1t = vt[:, K * G:2 * K * G, :].rearrange("p n t -> p (n t)")
+        NS = K * G * T
+        sgn = keep.tile([P, NS], F32, name="sgn")
+        mag = keep.tile([P, NS], F32, name="mag")
+        rb = keep.tile([P, NS], F32, name="rb")
+
+        xi = {}
+        xc = {}
+
+        def xr_mul(u):
+            c, k = divmod(u, K)
+            t = work.tile([P, N, T], BF16, name="xr", align_bytes=64)
+            xi[u] = t
+            nc.vector.tensor_tensor(out=t[:], in0=xT[c][:], in1=vt[:, 2 * K * G + k, :].unsqueeze(1).to_broadcast([P, N, T]), op=ALU.mult)
+
+        def xr_quant(u):
+            codes = work.tile([P, N], U32, name="xc", align_bytes=64)
+            scales = work.tile([P, N], U8, name="xs", align_bytes=64)
+            nc.vector.quantize_mx(out=codes[:].bitcast(FP8X4), scales=scales[:], in_=xi.pop(u)[:].rearrange("p n t -> p (n t)"))
+            xc[u] = (codes, scales)
+
+        xr_mul(0)
+        w1_inter(0, nc.vector.tensor_copy)
+        xr_quant(0)
+        nc.vector.tensor_scalar(out=sgn[:], in0=r2t, scalar1=0.0, scalar2=2.0, op0=ALU.is_ge, op1=ALU.mult)
+        w1_quant(0)
+        nc.vector.tensor_scalar(out=sgn[:], in0=sgn[:], scalar1=-1.0, scalar2=None, op0=ALU.add)
+        w1_inter(1, nc.scalar.copy)
+        nc.vector.tensor_tensor(out=mag[:], in0=sgn[:], in1=r2t, op=ALU.mult)
+        nc.vector.tensor_tensor(out=rb[:], in0=mag[:], in1=b1t, op=ALU.mult)
+
+        w2p = [keep.tile([P, T, C], BF16, name="w2p%d" % g, align_bytes=64) for g in range(G)]
+        w2i = [keep.tile([P, C, T], BF16, name="w2i%d" % g, align_bytes=64) for g in range(G)]
+        w2c = [keep.tile([P, C], U32, name="w2c%d" % g, align_bytes=64) for g in range(G)]
+        w2q = [keep.tile([P, C], U8, name="w2q%d" % g, align_bytes=64) for g in range(G)]
+
+        def w2_widen(g, t):
+            nc.scalar.activation(out=w2p[g][:, t, :], in_=w2raw[:, g, t, :].bitcast(FP8), func=ACT.Copy, scale=w2s[:, g, t:t + 1])
+
+        def interleave(copy, dst, src):
+            copy(out=dst.rearrange("p (c i) t -> p c t i", i=4), in_=src.rearrange("p t (c i) -> p c t i", i=4))
+
+        def w2_quant(g):
+            nc.vector.quantize_mx(out=w2c[g][:].bitcast(FP8X4), scales=w2q[g][:], in_=w2i[g][:].rearrange("p n t -> p (n t)"))
+
+        abank = {}
+        plane = {}
+        hi = {}
+        hc = {}
+
+        def col(h, t):
+            k, g = divmod(h % (K * G), G)
+            return (k * G + g) * T + t
+
+        def mm(h):
+            u, g = divmod(h, G)
+            codes, scales = xc[u]
+            for t in range(T):
+                if t % 2 == 0:
+                    bank = ps_a.tile([P, 2, N], F32, name="a", tag="a")
+                    abank[h, t // 2] = bank
+                cols = slice(t * P, (t + 1) * P)
+                nc.tensor.matmul_mx(out=bank[:, t % 2, :], lhsT=w1c[g][:, cols].bitcast(FP8X4), lhsT_scale=w1s[g][:, cols],
+                                    rhs=codes[:].bitcast(FP8X4), rhs_scale=scales[:], start=True, stop=True)
+
+        def relu(h):
+            pl = work.tile([P, T, N], BF16, name="pl", align_bytes=64)
+            plane[h] = pl
+            for t in range(T):
+                j = col(h, t)
+                nc.scalar.activation(out=pl[:, t, :], in_=abank[h, t // 2][:, t % 2, :], func=ACT.Relu,
+                                     bias=rb[:, j:j + 1], scale=mag[:, j:j + 1])
+
+        def flips(h):
+            for t in range(T):
+                j = col(h, t)
+                nc.vector.tensor_scalar(out=plane[h][:, t, :], in0=plane[h][:, t, :], scalar1=sgn[:, j:j + 1], scalar2=None, op0=ALU.mult)
+
+        def inter(h, copy):
+            t = work.tile([P, N, T], BF16, name="hi", align_bytes=64)
+            hi[h] = t
+            interleave(copy, t[:], plane.pop(h)[:])
+
+        def quant(h):
+            c, r = divmod(h, K * G)
+            codes = two.tile([P, N], U32, name="hc%d" % r, align_bytes=64)
+            scales = two.tile([P, N], U8, name="hs%d" % r, align_bytes=64)
+            nc.vector.quantize_mx(out=codes[:].bitcast(FP8X4), scales=scales[:], in_=hi.pop(h)[:].rearrange("p n t -> p (n t)"))
+            hc[h] = (codes, scales)
+
+        psb = keep.tile([P, NT, C], F32, name="psb", align_bytes=64)
+        tn = [keep.tile([P, C], BF16, name="tn%d" % i, align_bytes=64) for i in range(NT)]
+        st = {}
+
+        def logits(i):
+            c, j = divmod(i, CH)
+            cols = slice(j * P, (j + 1) * P)
+            s = {}
+            st[i] = s
+            s["l"] = []
+            for k in range(K):
+                bank = ps_l.tile([P, C], F32, name="l%d" % k)
+                s["l"].append(bank)
+                for g in range(G):
+                    codes, scales = hc[(c * K + k) * G + g]
+                    nc.tensor.matmul_mx(out=bank[:], lhsT=codes[:, cols].bitcast(FP8X4), lhsT_scale=scales[:, cols],
+                                        rhs=w2c[g][:].bitcast(FP8X4), rhs_scale=w2q[g][:], start=(g == 0), stop=(g == G - 1))
+            s["lb"] = two.tile([P, K, C], BF16, name="lb", align_bytes=64)
+            s["nm"] = two.tile([P, K], F32, name="nm")
+            s["sum"] = two.tile([P, K], F32, name="sum")
+            s["w"] = two.tile([P, K], F32, name="w")
+            s["d"] = two.tile([P, K, C], F32, name="d", align_bytes=64)
+            s["dg"] = two.tile([P, K, P], F32, name="dg", align_bytes=64)
+
+        def rowmax(i, k):
+            s = st[i]
+            nc.vector.tensor_scalar(out=s["lb"][:, k, :], in0=s["l"][k][:], scalar1=-1.0, scalar2=None, op0=ALU.mult, op1=ALU.min,
+                                    accum_out=s["nm"][:, k:k + 1])
+
+        def expsum(i, k):
+            s = st[i]
+            junk = two.tile([P, C], BF16, name="junk", align_bytes=64)
+            nc.scalar.activation(out=junk[:], in_=s["l"][k][:], func=ACT.Exp, bias=s["nm"][:, k:k + 1], accum_out=s["sum"][:, k:k + 1])
+
+        def center(i, k):
+            s = st[i]
+            nc.vector.tensor_scalar(out=s["lb"][:, k, :], in0=s["lb"][:, k, :], scalar1=s["nm"][:, k:k + 1], scalar2=None, op0=ALU.subtract)
+
+        def min4(i):
+            lb = st[i]["lb"]
+            nc.vector.tensor_tensor(out=lb[:, 0:2, :], in0=lb[:, 0:2, :], in1=lb[:, 2:4, :], op=ALU.min)
+
+        def min2(i):
+            lb = st[i]["lb"]
+            nc.vector.tensor_tensor(out=tn[i][:], in0=lb[:, 0, :], in1=lb[:, 1, :], op=ALU.min)
+
+        def shift(i, k):
+            s = st[i]
+            nc.vector.scalar_tensor_tensor(out=s["d"][:, k, :], in0=s["l"][k][:], scalar=s["nm"][:, k:k + 1], in1=tn[i][:], op0=ALU.add, op1=ALU.add)
+
+        def exps(i, k):
+            d = st[i]["d"][:, k:k + 2, :]
+            nc.scalar.activation(out=d, in_=d, func=ACT.Exp)
+
+        def weights(i):
+            s = st[i]
+            nc.vector.reciprocal(out=s["w"][:], in_=s["sum"][:])
+
+        def diag(i):
+            s = st[i]
+            for k in range(K):
+                nc.vector.tensor_scalar(out=s["dg"][:, k, :], in0=ident[:], scalar1=s["w"][:, k:k + 1], scalar2=None, op0=ALU.mult)
+
+        def mix(i, k):
+            s = st[i]
+            if k == 0:
+                s["p"] = ps_l.tile([P, C], F32, name="mix")
+            nc.tensor.matmul(out=s["p"][:], lhsT=s["dg"][:, k, :], rhs=s["d"][:, k, :], start=(k == 0), stop=(k == K - 1))
+
+        def park(i):
+            nc.scalar.copy(out=psb[:, i, :], in_=st[i]["p"][:])
+
+        def s2_pe(i, q):
+            if q == 4:
+                mix(i, 0)
+                mix(i, 1)
+            if q == 5:
+                mix(i, 2)
+                mix(i, 3)
+
+        def s2_vec(i, q):
+            if q == 0:
+                return [lambda: rowmax(i, 0), lambda: rowmax(i, 1)]
+            if q == 1:
+                return [lambda: rowmax(i, 2), lambda: center(i, 0), lambda: rowmax(i, 3), lambda: center(i, 1)]
+            if q == 2:
+                return [lambda: center(i, 2), lambda: center(i, 3), lambda: min4(i), lambda: min2(i), lambda: shift(i, 0), lambda: shift(i, 1)]
+            if q == 3:
+                return [lambda: shift(i, 2), lambda: weights(i), lambda: shift(i, 3), lambda: diag(i)]
+            return []
+
+        def s2_act(i, q):
+            if q == 0:
+                expsum(i, 0)
+            if q == 1:
+                expsum(i, 1)
+                expsum(i, 2)
+            if q == 2:
+                expsum(i, 3)
+            if q == 3:
+                exps(i, 0)
+            if q == 4:
+                exps(i, 2)
+            if q == 6:
+                park(i)
+
+        start = {}
+        for i in range(NT):
+            start[i] = (i // CH) * K * G + K * G + 2 + 4 * (i % CH)
+        last = start[NT - 1] + 6
+
+        for tau in range(last + 1):
+            live = [(i, tau - start[i]) for i in range(NT) if 0 <= tau - start[i] <= 6]
+            if 0 <= tau - 3 < NH and tau in start.values():
+                quant(tau - 3)
+            for i, q in live:
+                if q == 0:
+                    logits(i)
+            if tau < NH:
+                mm(tau)
+            if 0 <= tau - 1 < NH:
+                relu(tau - 1)
+            vec_work = []
+            for i, q in live:
+                vec_work += s2_vec(i, q)
+            if 0 <= tau - 2 < NH:
+                flips(tau - 2)
+            if 0 <= tau - 3 < NH and tau not in start.values():
+                quant(tau - 3)
+            if tau == 0:
+                w1_quant(1)
+            if vec_work:
+                vec_work.pop(0)()
+            u = (tau + 1) // 2
+            if tau % 2 == 1 and u < NCH * K:
+                xr_mul(u)
+            if 0 <= tau - 2 < NH:
+                on_act = vec_work and tau % 2 == 1
+                inter(tau - 2, nc.scalar.copy if on_act else nc.vector.tensor_copy)
+            if vec_work:
+                vec_work.pop(0)()
+            if tau % 2 == 1 and u < NCH * K:
+                xr_quant(u)
+            for f in vec_work:
+                f()
+            for i, q in live:
+                s2_act(i, q)
+            for i, q in live:
+                s2_pe(i, q)
+            if tau in (2, 5):
+                turn_x(1 + (tau - 2) // 3)
+            if tau < 8:
+                w2_widen(tau // 4, tau % 4)
+            if tau in (5, 8):
+                g = (tau - 5) // 3
+                interleave(nc.vector.tensor_copy, w2i[g][:], w2p[g][:])
+            if tau in (6, 9):
+                w2_quant((tau - 6) // 3)
+
+        for i in range(NT):
+            lnv = two.tile([P, C], F32, name="lnv", align_bytes=64)
+            nc.scalar.activation(out=lnv[:], in_=psb[:, i, :], func=ACT.Ln, scale=float(C) / K)
+            o = two.tile([P, C], F32, name="o", align_bytes=64)
+            nc.vector.tensor_tensor(out=o[:], in0=lnv[:], in1=tn[i][:], op=ALU.subtract)
+            nc.sync.dma_start(out=ov[:, i, :], in_=o[:])

@@ -19,10 +19,13 @@ P = 128
 T = 4
 G = H // (P * T)
 NT = B // P
-CH = 2
-N = CH * P
-NCH = NT // CH
-NH = NCH * K * G
+CHUNKS = ((0, 4), (4, 2))
+NCH = len(CHUNKS)
+KG = K * G
+NH = NCH * KG
+BANK = 512
+FIRST_HELD = 3
+ON_ACT = (0, 3, 6, 8, 10, 12, 14)
 
 
 def tile_tabmbatchensemblelogmeanprob_kernel(tc, x, r1, w1, b1, r2, w2_bytes, w2_scale, out):
@@ -33,7 +36,6 @@ def tile_tabmbatchensemblelogmeanprob_kernel(tc, x, r1, w1, b1, r2, w2_bytes, w2
         two = ctx.enter_context(tc.tile_pool(name="two", bufs=2))
         ps_a = ctx.enter_context(tc.psum_pool(name="ps_a", bufs=3))
         ps_l = ctx.enter_context(tc.psum_pool(name="ps_l", bufs=1))
-        ctx.enter_context(tc.manual_schedule())
 
         vec = keep.tile([P, T * P], BF16, name="vec", align_bytes=64)
         nc.vector.memset(vec[:], 0.0)
@@ -46,34 +48,36 @@ def tile_tabmbatchensemblelogmeanprob_kernel(tc, x, r1, w1, b1, r2, w2_bytes, w2
 
         xv = x.rearrange("(p i) d -> p i d", i=NT)
         ov = out.rearrange("(p i) c -> p i c", i=NT)
-        xraw = [keep.tile([P, CH, D], BF16, name="xraw%d" % c, align_bytes=64) for c in range(NCH)]
+        xraw = [keep.tile([P, 2, D], BF16, name="xraw%d" % e, align_bytes=64) for e in range(NT // 2)]
         w1raw = [keep.tile([P, T, P * T], BF16, name="w1raw%d" % g, align_bytes=64) for g in range(G)]
         w1v = w1.rearrange("(p j) h -> p j h", j=T)
-        nc.sync.dma_start(out=xraw[0][:], in_=xv[:, 0:CH, :])
-        nc.sync.dma_start(out=w1raw[0][:], in_=w1v[:, :, 0:P * T])
+        nc.sync.dma_start(out=xraw[0][:], in_=xv[:, 0:2, :])
         nc.sync.dma_start(out=vec[16:20, :], in_=r1)
         nc.sync.dma_start(out=vec[0:8, :], in_=r2.rearrange("k (g c) -> (k g) c", g=G))
         nc.sync.dma_start(out=vec[8:16, :], in_=b1.rearrange("k (g c) -> (k g) c", g=G))
+        nc.sync.dma_start(out=w1raw[0][:], in_=w1v[:, :, 0:P * T])
+        nc.sync.dma_start(out=xraw[1][:], in_=xv[:, 2:4, :])
         nc.sync.dma_start(out=w1raw[1][:], in_=w1v[:, :, P * T:2 * P * T])
-        for c in range(1, NCH):
-            nc.sync.dma_start(out=xraw[c][:], in_=xv[:, c * CH:(c + 1) * CH, :])
+        nc.sync.dma_start(out=xraw[2][:], in_=xv[:, 4:6, :])
         w2raw = keep.tile([P, G, T, C], U8, name="w2raw", align_bytes=64)
         nc.sync.dma_start(out=w2raw[:], in_=w2_bytes.rearrange("(g p t) n -> p g t n", p=P, t=T))
         w2s = keep.tile([P, G, T], F32, name="w2s")
         nc.sync.dma_start(out=w2s[:], in_=w2_scale.rearrange("(g p t) o -> p g (t o)", p=P, t=T))
 
-        xT = [keep.tile([P, N, T], BF16, name="xT%d" % c, align_bytes=64) for c in range(NCH)]
+        xT = [keep.tile([P, m * P, T], BF16, name="xT%d" % c, align_bytes=64) for c, (i0, m) in enumerate(CHUNKS)]
 
-        def turn_x(c):
-            bank = ps_a.tile([P, CH, 2, P], F32, name="xbank", tag="a")
-            for i in range(CH):
-                words = xraw[c][:, i, :].bitcast(F32)
+        def turn_x(e, copy):
+            c = 1 if 2 * e >= CHUNKS[1][0] else 0
+            n0 = (2 * e - CHUNKS[c][0]) * P
+            bank = ps_a.tile([P, 2, 2, P], F32, name="xbank", tag="a")
+            for i in range(2):
+                words = xraw[e][:, i, :].bitcast(F32)
                 for u in range(2):
                     nc.tensor.transpose(bank[:, i, u, :], words[:, u:2 * P:2], ident[:])
-            xw = xT[c][:].rearrange("p n t -> p (n t)").bitcast(F32)
-            nc.scalar.copy(out=xw.rearrange("p (i r u) -> p i r u", i=CH, u=2), in_=bank[:].rearrange("p i u r -> p i r u"))
+            xw = xT[c][:, n0:n0 + 2 * P, :].rearrange("p n t -> p (n t)").bitcast(F32)
+            copy(out=xw.rearrange("p (i r u) -> p i r u", i=2, u=2), in_=bank[:].rearrange("p i u r -> p i r u"))
 
-        turn_x(0)
+        turn_x(0, nc.scalar.copy)
         vbank = ps_a.tile([P, 2, P], F32, name="vbank", tag="a")
         vwords = vec[:].bitcast(F32)
         for u in range(2):
@@ -107,23 +111,26 @@ def tile_tabmbatchensemblelogmeanprob_kernel(tc, x, r1, w1, b1, r2, w2_bytes, w2
 
         def xr_mul(u):
             c, k = divmod(u, K)
-            t = work.tile([P, N, T], BF16, name="xr", align_bytes=64)
+            n = CHUNKS[c][1] * P
+            t = work.tile([P, n, T], BF16, name="xr", align_bytes=64)
             xi[u] = t
-            nc.vector.tensor_tensor(out=t[:], in0=xT[c][:], in1=vt[:, 2 * K * G + k, :].unsqueeze(1).to_broadcast([P, N, T]), op=ALU.mult)
+            nc.vector.tensor_tensor(out=t[:], in0=xT[c][:], in1=vt[:, 2 * KG + k, :].unsqueeze(1).to_broadcast([P, n, T]), op=ALU.mult)
 
         def xr_quant(u):
-            codes = work.tile([P, N], U32, name="xc", align_bytes=64)
-            scales = work.tile([P, N], U8, name="xs", align_bytes=64)
+            n = CHUNKS[u // K][1] * P
+            codes = work.tile([P, n], U32, name="xc", align_bytes=64)
+            scales = work.tile([P, n], U8, name="xs", align_bytes=64)
             nc.vector.quantize_mx(out=codes[:].bitcast(FP8X4), scales=scales[:], in_=xi.pop(u)[:].rearrange("p n t -> p (n t)"))
             xc[u] = (codes, scales)
 
-        xr_mul(0)
         w1_inter(0, nc.vector.tensor_copy)
-        xr_quant(0)
-        nc.vector.tensor_scalar(out=sgn[:], in0=r2t, scalar1=0.0, scalar2=2.0, op0=ALU.is_ge, op1=ALU.mult)
         w1_quant(0)
+        turn_x(1, nc.scalar.copy)
+        nc.vector.tensor_scalar(out=sgn[:], in0=r2t, scalar1=0.0, scalar2=2.0, op0=ALU.is_ge, op1=ALU.mult)
+        xr_mul(0)
         nc.vector.tensor_scalar(out=sgn[:], in0=sgn[:], scalar1=-1.0, scalar2=None, op0=ALU.add)
         w1_inter(1, nc.scalar.copy)
+        xr_quant(0)
         nc.vector.tensor_tensor(out=mag[:], in0=sgn[:], in1=r2t, op=ALU.mult)
         nc.vector.tensor_tensor(out=rb[:], in0=mag[:], in1=b1t, op=ALU.mult)
 
@@ -147,26 +154,28 @@ def tile_tabmbatchensemblelogmeanprob_kernel(tc, x, r1, w1, b1, r2, w2_bytes, w2
         hc = {}
 
         def col(h, t):
-            k, g = divmod(h % (K * G), G)
-            return (k * G + g) * T + t
+            return h % KG * T + t
 
         def mm(h):
             u, g = divmod(h, G)
             codes, scales = xc[u]
+            n = CHUNKS[u // K][1] * P
+            per = BANK // n
             for t in range(T):
-                if t % 2 == 0:
-                    bank = ps_a.tile([P, 2, N], F32, name="a", tag="a")
-                    abank[h, t // 2] = bank
+                if t % per == 0:
+                    bank = ps_a.tile([P, per, n], F32, name="a", tag="a")
+                abank[h, t] = bank[:, t % per, :]
                 cols = slice(t * P, (t + 1) * P)
-                nc.tensor.matmul_mx(out=bank[:, t % 2, :], lhsT=w1c[g][:, cols].bitcast(FP8X4), lhsT_scale=w1s[g][:, cols],
+                nc.tensor.matmul_mx(out=abank[h, t], lhsT=w1c[g][:, cols].bitcast(FP8X4), lhsT_scale=w1s[g][:, cols],
                                     rhs=codes[:].bitcast(FP8X4), rhs_scale=scales[:], start=True, stop=True)
 
         def relu(h):
-            pl = work.tile([P, T, N], BF16, name="pl", align_bytes=64)
+            n = CHUNKS[h // KG][1] * P
+            pl = work.tile([P, T, n], BF16, name="pl", align_bytes=64)
             plane[h] = pl
             for t in range(T):
                 j = col(h, t)
-                nc.scalar.activation(out=pl[:, t, :], in_=abank[h, t // 2][:, t % 2, :], func=ACT.Relu,
+                nc.scalar.activation(out=pl[:, t, :], in_=abank.pop((h, t)), func=ACT.Relu,
                                      bias=rb[:, j:j + 1], scale=mag[:, j:j + 1])
 
         def flips(h):
@@ -175,14 +184,15 @@ def tile_tabmbatchensemblelogmeanprob_kernel(tc, x, r1, w1, b1, r2, w2_bytes, w2
                 nc.vector.tensor_scalar(out=plane[h][:, t, :], in0=plane[h][:, t, :], scalar1=sgn[:, j:j + 1], scalar2=None, op0=ALU.mult)
 
         def inter(h, copy):
-            t = work.tile([P, N, T], BF16, name="hi", align_bytes=64)
+            t = work.tile([P, CHUNKS[h // KG][1] * P, T], BF16, name="hi", align_bytes=64)
             hi[h] = t
             interleave(copy, t[:], plane.pop(h)[:])
 
         def quant(h):
-            c, r = divmod(h, K * G)
-            codes = two.tile([P, N], U32, name="hc%d" % r, align_bytes=64)
-            scales = two.tile([P, N], U8, name="hs%d" % r, align_bytes=64)
+            c, r = divmod(h, KG)
+            n = CHUNKS[c][1] * P
+            codes = two.tile([P, n], U32, name="hc%d" % r, align_bytes=64)
+            scales = two.tile([P, n], U8, name="hs%d" % r, align_bytes=64)
             nc.vector.quantize_mx(out=codes[:].bitcast(FP8X4), scales=scales[:], in_=hi.pop(h)[:].rearrange("p n t -> p (n t)"))
             hc[h] = (codes, scales)
 
@@ -191,7 +201,8 @@ def tile_tabmbatchensemblelogmeanprob_kernel(tc, x, r1, w1, b1, r2, w2_bytes, w2
         st = {}
 
         def logits(i):
-            c, j = divmod(i, CH)
+            c = 1 if i >= CHUNKS[1][0] else 0
+            j = i - CHUNKS[c][0]
             cols = slice(j * P, (j + 1) * P)
             s = {}
             st[i] = s
@@ -200,7 +211,7 @@ def tile_tabmbatchensemblelogmeanprob_kernel(tc, x, r1, w1, b1, r2, w2_bytes, w2
                 bank = ps_l.tile([P, C], F32, name="l%d" % k)
                 s["l"].append(bank)
                 for g in range(G):
-                    codes, scales = hc[(c * K + k) * G + g]
+                    codes, scales = hc[c * KG + k * G + g]
                     nc.tensor.matmul_mx(out=bank[:], lhsT=codes[:, cols].bitcast(FP8X4), lhsT_scale=scales[:, cols],
                                         rhs=w2c[g][:].bitcast(FP8X4), rhs_scale=w2q[g][:], start=(g == 0), stop=(g == G - 1))
             s["lb"] = two.tile([P, K, C], BF16, name="lb", align_bytes=64)
@@ -236,8 +247,8 @@ def tile_tabmbatchensemblelogmeanprob_kernel(tc, x, r1, w1, b1, r2, w2_bytes, w2
             s = st[i]
             nc.vector.scalar_tensor_tensor(out=s["d"][:, k, :], in0=s["l"][k][:], scalar=s["nm"][:, k:k + 1], in1=tn[i][:], op0=ALU.add, op1=ALU.add)
 
-        def exps(i, k):
-            d = st[i]["d"][:, k:k + 2, :]
+        def exps(i, k, m):
+            d = st[i]["d"][:, k:k + m, :]
             nc.scalar.activation(out=d, in_=d, func=ACT.Exp)
 
         def weights(i):
@@ -247,107 +258,133 @@ def tile_tabmbatchensemblelogmeanprob_kernel(tc, x, r1, w1, b1, r2, w2_bytes, w2
         def diag(i):
             s = st[i]
             for k in range(K):
-                nc.vector.tensor_scalar(out=s["dg"][:, k, :], in0=ident[:], scalar1=s["w"][:, k:k + 1], scalar2=None, op0=ALU.mult)
+                nc.gpsimd.tensor_scalar(out=s["dg"][:, k, :], in0=ident[:], scalar1=s["w"][:, k:k + 1], scalar2=1.0, op0=ALU.mult, op1=ALU.mult)
 
         def mix(i, k):
             s = st[i]
             if k == 0:
-                s["p"] = ps_l.tile([P, C], F32, name="mix")
+                s["p"] = ps_l.tile([P, C], F32, name="mix") if i < FIRST_HELD else ps_a.tile([P, C], F32, name="held", tag="a")
             nc.tensor.matmul(out=s["p"][:], lhsT=s["dg"][:, k, :], rhs=s["d"][:, k, :], start=(k == 0), stop=(k == K - 1))
 
         def park(i):
             nc.scalar.copy(out=psb[:, i, :], in_=st[i]["p"][:])
 
-        def s2_pe(i, q):
-            if q == 4:
-                mix(i, 0)
-                mix(i, 1)
-            if q == 5:
-                mix(i, 2)
-                mix(i, 3)
-
         def s2_vec(i, q):
             if q == 0:
-                return [lambda: rowmax(i, 0), lambda: rowmax(i, 1)]
+                return [(rowmax, i, 0), (rowmax, i, 1)]
             if q == 1:
-                return [lambda: rowmax(i, 2), lambda: center(i, 0), lambda: rowmax(i, 3), lambda: center(i, 1)]
+                return [(rowmax, i, 2), (center, i, 0), (rowmax, i, 3), (center, i, 1)]
             if q == 2:
-                return [lambda: center(i, 2), lambda: center(i, 3), lambda: min4(i), lambda: min2(i), lambda: shift(i, 0), lambda: shift(i, 1)]
+                return [(center, i, 2), (center, i, 3), (min4, i), (min2, i), (shift, i, 0), (shift, i, 1)]
             if q == 3:
-                return [lambda: shift(i, 2), lambda: weights(i), lambda: shift(i, 3), lambda: diag(i)]
+                return [(shift, i, 2), (shift, i, 3)]
             return []
 
         def s2_act(i, q):
             if q == 0:
-                expsum(i, 0)
+                return [(expsum, i, 0)]
             if q == 1:
-                expsum(i, 1)
-                expsum(i, 2)
+                return [(expsum, i, 1), (expsum, i, 2)]
             if q == 2:
-                expsum(i, 3)
+                return [(expsum, i, 3)]
             if q == 3:
-                exps(i, 0)
+                return [(exps, i, 0, 2)]
             if q == 4:
-                exps(i, 2)
-            if q == 6:
-                park(i)
+                return [(exps, i, 2, 2)] if i < NT - 1 else [(exps, i, 2, 1), (exps, i, 3, 1)]
+            if q == 6 and i < FIRST_HELD:
+                return [(park, i)]
+            return []
+
+        def spread(a, b):
+            o = []
+            done = 0
+            for n, f in enumerate(a):
+                o.append(f)
+                want = (n + 1) * len(b) // len(a)
+                while done < want:
+                    o.append(b[done])
+                    done += 1
+            return o + list(b[done:])
+
+        def run(fs):
+            for f in fs:
+                f[0](*f[1:])
 
         start = {}
         for i in range(NT):
-            start[i] = (i // CH) * K * G + K * G + 2 + 4 * (i % CH)
-        last = start[NT - 1] + 6
+            start[i] = KG + 2 + 2 * i
+        last = start[NT - 1] + 2
+
+        def w2_inter(g):
+            interleave(nc.vector.tensor_copy, w2i[g][:], w2p[g][:])
 
         for tau in range(last + 1):
-            live = [(i, tau - start[i]) for i in range(NT) if 0 <= tau - start[i] <= 6]
-            if 0 <= tau - 3 < NH and tau in start.values():
-                quant(tau - 3)
+            live = []
+            for i in range(NT):
+                for q in (2 * (tau - start[i]), 2 * (tau - start[i]) + 1):
+                    if 0 <= q <= 6:
+                        live.append((i, q))
+            begins = tau in start.values()
+            v1 = []
+            if 0 <= tau - 2 < NH:
+                v1.append((flips, tau - 2))
+            if 0 <= tau - 3 < NH:
+                if begins:
+                    quant(tau - 3)
+                else:
+                    v1.append((quant, tau - 3))
             for i, q in live:
                 if q == 0:
                     logits(i)
             if tau < NH:
                 mm(tau)
+            u = (tau + 1) // 2
+            fresh = tau % 2 == 1 and u < NCH * K
+            if tau == 0:
+                v1.append((w1_quant, 1))
+            if fresh:
+                v1.append((xr_mul, u))
+            on_act = tau - 2 in ON_ACT
+            if 0 <= tau - 2 < NH and not on_act:
+                v1.append((inter, tau - 2, nc.vector.tensor_copy))
+            if fresh:
+                v1.append((xr_quant, u))
+            if tau in (5, 8):
+                v1.append((w2_inter, (tau - 5) // 3))
+            if tau in (6, 9):
+                v1.append((w2_quant, (tau - 6) // 3))
+            v2 = []
+            for i, q in live:
+                v2 += s2_vec(i, q)
+            a1 = []
             if 0 <= tau - 1 < NH:
                 relu(tau - 1)
-            vec_work = []
+            run(spread(v2, v1) if v2 else v1)
+            a2 = []
             for i, q in live:
-                vec_work += s2_vec(i, q)
-            if 0 <= tau - 2 < NH:
-                flips(tau - 2)
-            if 0 <= tau - 3 < NH and tau not in start.values():
-                quant(tau - 3)
-            if tau == 0:
-                w1_quant(1)
-            if vec_work:
-                vec_work.pop(0)()
-            u = (tau + 1) // 2
-            if tau % 2 == 1 and u < NCH * K:
-                xr_mul(u)
-            if 0 <= tau - 2 < NH:
-                on_act = vec_work and tau % 2 == 1
-                inter(tau - 2, nc.scalar.copy if on_act else nc.vector.tensor_copy)
-            if vec_work:
-                vec_work.pop(0)()
-            if tau % 2 == 1 and u < NCH * K:
-                xr_quant(u)
-            for f in vec_work:
-                f()
+                a2 += s2_act(i, q)
+            if 0 <= tau - 2 < NH and on_act:
+                a1.append((inter, tau - 2, nc.scalar.copy))
+            run(spread(a2, a1) if a2 else a1)
             for i, q in live:
-                s2_act(i, q)
-            for i, q in live:
-                s2_pe(i, q)
-            if tau in (2, 5):
-                turn_x(1 + (tau - 2) // 3)
+                if q == 3:
+                    weights(i)
+                    diag(i)
+                    mix(i, 0)
+                    mix(i, 1)
+                if q == 4:
+                    mix(i, 2)
+                    mix(i, 3)
+            if tau == 3:
+                turn_x(2, nc.scalar.copy)
             if tau < 8:
                 w2_widen(tau // 4, tau % 4)
-            if tau in (5, 8):
-                g = (tau - 5) // 3
-                interleave(nc.vector.tensor_copy, w2i[g][:], w2p[g][:])
-            if tau in (6, 9):
-                w2_quant((tau - 6) // 3)
 
+        factor = keep.tile([P, 1], F32, name="factor")
+        nc.vector.tensor_scalar(out=factor[:], in0=st[NT - 1]["d"][:, K - 1, C - 1:C], scalar1=0.0, scalar2=float(C) / K, op0=ALU.mult, op1=ALU.add)
         for i in range(NT):
-            lnv = two.tile([P, C], F32, name="lnv", align_bytes=64)
-            nc.scalar.activation(out=lnv[:], in_=psb[:, i, :], func=ACT.Ln, scale=float(C) / K)
-            o = two.tile([P, C], F32, name="o", align_bytes=64)
-            nc.vector.tensor_tensor(out=o[:], in0=lnv[:], in1=tn[i][:], op=ALU.subtract)
+            src = psb[:, i, :] if i < FIRST_HELD else st[i]["p"][:]
+            nc.scalar.activation(out=psb[:, i, :], in_=src, func=ACT.Ln, scale=factor[:])
+            o = keep.tile([P, C], F32, name="o%d" % i, align_bytes=64)
+            nc.vector.tensor_tensor(out=o[:], in0=psb[:, i, :], in1=tn[i][:], op=ALU.subtract)
             nc.sync.dma_start(out=ov[:, i, :], in_=o[:])

from contextlib import ExitStack

import concourse.mybir as mybir
from concourse.masks import make_identity

B, K, D, H, C = 768, 4, 512, 1024, 512
FLOPS = 2 * K * B * (D * H + H * C)

F32 = mybir.dt.float32
BF16 = mybir.dt.bfloat16
U32 = mybir.dt.uint32
U8 = mybir.dt.uint8
FP8 = mybir.dt.float8_e4m3fn
FP8X4 = mybir.dt.float8_e4m3fn_x4
ALU = mybir.AluOpType
ACT = mybir.ActivationFunctionType

P = 128
T = 4
G = H // (P * T)
NT = B // P
CHUNKS = ((0, 4), (4, 2))
NCH = len(CHUNKS)
KG = K * G
NH = NCH * KG
BANK = 512
FIRST_HELD = 3
ON_ACT = (0, 3, 6, 8, 10, 12, 14)


def tile_tabmbatchensemblelogmeanprob_kernel(tc, x, r1, w1, b1, r2, w2_bytes, w2_scale, out):
    nc = tc.nc
    with ExitStack() as ctx:
        keep = ctx.enter_context(tc.tile_pool(name="keep", bufs=1))
        work = ctx.enter_context(tc.tile_pool(name="work", bufs=3))
        two = ctx.enter_context(tc.tile_pool(name="two", bufs=2))
        ps_a = ctx.enter_context(tc.psum_pool(name="ps_a", bufs=3))
        ps_l = ctx.enter_context(tc.psum_pool(name="ps_l", bufs=1))

        vec = keep.tile([P, T * P], BF16, name="vec", align_bytes=64)
        nc.vector.memset(vec[:], 0.0)
        ident = keep.tile([P, P], F32, name="ident", align_bytes=64)
        make_identity(nc, ident[:])
        one = keep.tile([P, 1], F32, name="one")
        nc.gpsimd.memset(one[:], 0.0)
        dummy = keep.tile([P, 1], F32, name="dummy")
        nc.scalar.activation(out=dummy[:], in_=one[:], func=ACT.Exp)

        xv = x.rearrange("(p i) d -> p i d", i=NT)
        ov = out.rearrange("(p i) c -> p i c", i=NT)
        xraw = [keep.tile([P, 2, D], BF16, name="xraw%d" % e, align_bytes=64) for e in range(NT // 2)]
        w1raw = [keep.tile([P, T, P * T], BF16, name="w1raw%d" % g, align_bytes=64) for g in range(G)]
        w1v = w1.rearrange("(p j) h -> p j h", j=T)
        nc.sync.dma_start(out=xraw[0][:], in_=xv[:, 0:2, :])
        nc.sync.dma_start(out=vec[16:20, :], in_=r1)
        nc.sync.dma_start(out=vec[0:8, :], in_=r2.rearrange("k (g c) -> (k g) c", g=G))
        nc.sync.dma_start(out=vec[8:16, :], in_=b1.rearrange("k (g c) -> (k g) c", g=G))
        nc.sync.dma_start(out=w1raw[0][:], in_=w1v[:, :, 0:P * T])
        nc.sync.dma_start(out=xraw[1][:], in_=xv[:, 2:4, :])
        nc.sync.dma_start(out=w1raw[1][:], in_=w1v[:, :, P * T:2 * P * T])
        nc.sync.dma_start(out=xraw[2][:], in_=xv[:, 4:6, :])
        w2raw = keep.tile([P, G, T, C], U8, name="w2raw", align_bytes=64)
        nc.sync.dma_start(out=w2raw[:], in_=w2_bytes.rearrange("(g p t) n -> p g t n", p=P, t=T))
        w2s = keep.tile([P, G, T], F32, name="w2s")
        nc.sync.dma_start(out=w2s[:], in_=w2_scale.rearrange("(g p t) o -> p g (t o)", p=P, t=T))

        xT = [keep.tile([P, m * P, T], BF16, name="xT%d" % c, align_bytes=64) for c, (i0, m) in enumerate(CHUNKS)]

        def turn_x(e, copy):
            c = 1 if 2 * e >= CHUNKS[1][0] else 0
            n0 = (2 * e - CHUNKS[c][0]) * P
            bank = ps_a.tile([P, 2, 2, P], F32, name="xbank", tag="a")
            for i in range(2):
                words = xraw[e][:, i, :].bitcast(F32)
                for u in range(2):
                    nc.tensor.transpose(bank[:, i, u, :], words[:, u:2 * P:2], ident[:])
            xw = xT[c][:, n0:n0 + 2 * P, :].rearrange("p n t -> p (n t)").bitcast(F32)
            copy(out=xw.rearrange("p (i r u) -> p i r u", i=2, u=2), in_=bank[:].rearrange("p i u r -> p i r u"))

        turn_x(0, nc.scalar.copy)
        vbank = ps_a.tile([P, 2, P], F32, name="vbank", tag="a")
        vwords = vec[:].bitcast(F32)
        for u in range(2):
            nc.tensor.transpose(vbank[:, u, :], vwords[:, u:2 * P:2], ident[:])
        NV = 2 * K * G + K
        vt = keep.tile([P, NV, T], BF16, name="vt", align_bytes=64)
        vtw = vt[:].rearrange("p n t -> p (n t)").bitcast(F32)

        w1c = [keep.tile([P, P * T], U32, name="w1c%d" % g, align_bytes=64) for g in range(G)]
        w1s = [keep.tile([P, P * T], U8, name="w1s%d" % g, align_bytes=64) for g in range(G)]
        w1i = [keep.tile([P, P * T, T], BF16, name="w1i%d" % g, align_bytes=64) for g in range(G)]

        def w1_inter(g, copy):
            for t in range(0, T, 2):
                copy(out=w1i[g][:, t * P:(t + 2) * P, :].rearrange("p (t m) j -> p t m j", t=2),
                     in_=w1raw[g][:].rearrange("p j (m t) -> p t m j", t=T)[:, t:t + 2])

        def w1_quant(g):
            nc.vector.quantize_mx(out=w1c[g][:].bitcast(FP8X4), scales=w1s[g][:], in_=w1i[g][:].rearrange("p n j -> p (n j)"))

        nc.vector.tensor_copy(out=vtw.rearrange("p (n u) -> p n u", u=2), in_=vbank[:, :, 0:NV].rearrange("p u n -> p n u"))
        r2t = vt[:, 0:K * G, :].rearrange("p n t -> p (n t)")
        b1t = vt[:, K * G:2 * K * G, :].rearrange("p n t -> p (n t)")
        NS = K * G * T
        sgn = keep.tile([P, NS], F32, name="sgn")
        mag = keep.tile([P, NS], F32, name="mag")
        rb = keep.tile([P, NS], F32, name="rb")

        xi = {}
        xc = {}

        def xr_mul(u):
            c, k = divmod(u, K)
            n = CHUNKS[c][1] * P
            t = work.tile([P, n, T], BF16, name="xr", align_bytes=64)
            xi[u] = t
            nc.vector.tensor_tensor(out=t[:], in0=xT[c][:], in1=vt[:, 2 * KG + k, :].unsqueeze(1).to_broadcast([P, n, T]), op=ALU.mult)

        def xr_quant(u):
            n = CHUNKS[u // K][1] * P
            codes = work.tile([P, n], U32, name="xc", align_bytes=64)
            scales = work.tile([P, n], U8, name="xs", align_bytes=64)
            nc.vector.quantize_mx(out=codes[:].bitcast(FP8X4), scales=scales[:], in_=xi.pop(u)[:].rearrange("p n t -> p (n t)"))
            xc[u] = (codes, scales)

        w1_inter(0, nc.vector.tensor_copy)
        w1_quant(0)
        turn_x(1, nc.scalar.copy)
        nc.vector.tensor_scalar(out=sgn[:], in0=r2t, scalar1=0.0, scalar2=2.0, op0=ALU.is_ge, op1=ALU.mult)
        xr_mul(0)
        nc.vector.tensor_scalar(out=sgn[:], in0=sgn[:], scalar1=-1.0, scalar2=None, op0=ALU.add)
        w1_inter(1, nc.scalar.copy)
        xr_quant(0)
        nc.vector.tensor_tensor(out=mag[:], in0=sgn[:], in1=r2t, op=ALU.mult)
        nc.vector.tensor_tensor(out=rb[:], in0=mag[:], in1=b1t, op=ALU.mult)

        w2p = [keep.tile([P, T, C], BF16, name="w2p%d" % g, align_bytes=64) for g in range(G)]
        w2i = [keep.tile([P, C, T], BF16, name="w2i%d" % g, align_bytes=64) for g in range(G)]
        w2c = [keep.tile([P, C], U32, name="w2c%d" % g, align_bytes=64) for g in range(G)]
        w2q = [keep.tile([P, C], U8, name="w2q%d" % g, align_bytes=64) for g in range(G)]

        def w2_widen(g, t):
            nc.scalar.activation(out=w2p[g][:, t, :], in_=w2raw[:, g, t, :].bitcast(FP8), func=ACT.Copy, scale=w2s[:, g, t:t + 1])

        def interleave(copy, dst, src):
            copy(out=dst.rearrange("p (c i) t -> p c t i", i=4), in_=src.rearrange("p t (c i) -> p c t i", i=4))

        def w2_quant(g):
            nc.vector.quantize_mx(out=w2c[g][:].bitcast(FP8X4), scales=w2q[g][:], in_=w2i[g][:].rearrange("p n t -> p (n t)"))

        abank = {}
        plane = {}
        hi = {}
        hc = {}

        def col(h, t):
            return h % KG * T + t

        def mm(h):
            u, g = divmod(h, G)
            codes, scales = xc[u]
            n = CHUNKS[u // K][1] * P
            per = BANK // n
            for t in range(T):
                if t % per == 0:
                    bank = ps_a.tile([P, per, n], F32, name="a", tag="a")
                abank[h, t] = bank[:, t % per, :]
                cols = slice(t * P, (t + 1) * P)
                nc.tensor.matmul_mx(out=abank[h, t], lhsT=w1c[g][:, cols].bitcast(FP8X4), lhsT_scale=w1s[g][:, cols],
                                    rhs=codes[:].bitcast(FP8X4), rhs_scale=scales[:], start=True, stop=True)

        def relu(h):
            n = CHUNKS[h // KG][1] * P
            pl = work.tile([P, T, n], BF16, name="pl", align_bytes=64)
            plane[h] = pl
            for t in range(T):
                j = col(h, t)
                nc.scalar.activation(out=pl[:, t, :], in_=abank.pop((h, t)), func=ACT.Relu,
                                     bias=rb[:, j:j + 1], scale=mag[:, j:j + 1])

        def flips(h):
            for t in range(T):
                j = col(h, t)
                nc.vector.tensor_scalar(out=plane[h][:, t, :], in0=plane[h][:, t, :], scalar1=sgn[:, j:j + 1], scalar2=None, op0=ALU.mult)

        def inter(h, copy):
            t = work.tile([P, CHUNKS[h // KG][1] * P, T], BF16, name="hi", align_bytes=64)
            hi[h] = t
            interleave(copy, t[:], plane.pop(h)[:])

        def quant(h):
            c, r = divmod(h, KG)
            n = CHUNKS[c][1] * P
            codes = two.tile([P, n], U32, name="hc%d" % r, align_bytes=64)
            scales = two.tile([P, n], U8, name="hs%d" % r, align_bytes=64)
            nc.vector.quantize_mx(out=codes[:].bitcast(FP8X4), scales=scales[:], in_=hi.pop(h)[:].rearrange("p n t -> p (n t)"))
            hc[h] = (codes, scales)

        psb = keep.tile([P, NT, C], F32, name="psb", align_bytes=64)
        tn = [keep.tile([P, C], BF16, name="tn%d" % i, align_bytes=64) for i in range(NT)]
        st = {}

        def logits(i):
            c = 1 if i >= CHUNKS[1][0] else 0
            j = i - CHUNKS[c][0]
            cols = slice(j * P, (j + 1) * P)
            s = {}
            st[i] = s
            s["l"] = []
            for k in range(K):
                bank = ps_l.tile([P, C], F32, name="l%d" % k)
                s["l"].append(bank)
                for g in range(G):
                    codes, scales = hc[c * KG + k * G + g]
                    nc.tensor.matmul_mx(out=bank[:], lhsT=codes[:, cols].bitcast(FP8X4), lhsT_scale=scales[:, cols],
                                        rhs=w2c[g][:].bitcast(FP8X4), rhs_scale=w2q[g][:], start=(g == 0), stop=(g == G - 1))
            s["lb"] = two.tile([P, K, C], BF16, name="lb", align_bytes=64)
            s["nm"] = two.tile([P, K], F32, name="nm")
            s["sum"] = two.tile([P, K], F32, name="sum")
            s["w"] = two.tile([P, K], F32, name="w")
            s["d"] = two.tile([P, K, C], F32, name="d", align_bytes=64)
            s["dg"] = two.tile([P, K, P], F32, name="dg", align_bytes=64)

        def rowmax(i, k):
            s = st[i]
            nc.vector.tensor_scalar(out=s["lb"][:, k, :], in0=s["l"][k][:], scalar1=-1.0, scalar2=None, op0=ALU.mult, op1=ALU.min,
                                    accum_out=s["nm"][:, k:k + 1])

        def expsum(i, k):
            s = st[i]
            junk = two.tile([P, C], BF16, name="junk", align_bytes=64)
            nc.scalar.activation(out=junk[:], in_=s["l"][k][:], func=ACT.Exp, bias=s["nm"][:, k:k + 1], accum_out=s["sum"][:, k:k + 1])

        def center(i, k):
            s = st[i]
            nc.vector.tensor_scalar(out=s["lb"][:, k, :], in0=s["lb"][:, k, :], scalar1=s["nm"][:, k:k + 1], scalar2=None, op0=ALU.subtract)

        def min4(i):
            lb = st[i]["lb"]
            nc.vector.tensor_tensor(out=lb[:, 0:2, :], in0=lb[:, 0:2, :], in1=lb[:, 2:4, :], op=ALU.min)

        def min2(i):
            lb = st[i]["lb"]
            nc.vector.tensor_tensor(out=tn[i][:], in0=lb[:, 0, :], in1=lb[:, 1, :], op=ALU.min)

        def shift(i, k):
            s = st[i]
            nc.vector.scalar_tensor_tensor(out=s["d"][:, k, :], in0=s["l"][k][:], scalar=s["nm"][:, k:k + 1], in1=tn[i][:], op0=ALU.add, op1=ALU.add)

        def exps(i, k, m):
            d = st[i]["d"][:, k:k + m, :]
            nc.scalar.activation(out=d, in_=d, func=ACT.Exp)

        def weights(i):
            s = st[i]
            nc.vector.reciprocal(out=s["w"][:], in_=s["sum"][:])

        def diag(i):
            s = st[i]
            for k in range(K):
                nc.gpsimd.tensor_scalar(out=s["dg"][:, k, :], in0=ident[:], scalar1=s["w"][:, k:k + 1], scalar2=1.0, op0=ALU.mult, op1=ALU.mult)

        def mix(i, k):
            s = st[i]
            if k == 0:
                s["p"] = ps_l.tile([P, C], F32, name="mix") if i < FIRST_HELD else ps_a.tile([P, C], F32, name="held", tag="a")
            nc.tensor.matmul(out=s["p"][:], lhsT=s["dg"][:, k, :], rhs=s["d"][:, k, :], start=(k == 0), stop=(k == K - 1))

        def park(i):
            nc.scalar.copy(out=psb[:, i, :], in_=st[i]["p"][:])

        def s2_vec(i, q):
            if q == 0:
                return [(rowmax, i, 0), (rowmax, i, 1)]
            if q == 1:
                return [(rowmax, i, 2), (center, i, 0), (rowmax, i, 3), (center, i, 1)]
            if q == 2:
                return [(center, i, 2), (center, i, 3), (min4, i), (min2, i), (shift, i, 0), (shift, i, 1)]
            if q == 3:
                return [(shift, i, 2), (shift, i, 3)]
            return []

        def s2_act(i, q):
            if q == 0:
                return [(expsum, i, 0)]
            if q == 1:
                return [(expsum, i, 1), (expsum, i, 2)]
            if q == 2:
                return [(expsum, i, 3)]
            if q == 3:
                return [(exps, i, 0, 2)]
            if q == 4:
                return [(exps, i, 2, 2)] if i < NT - 1 else [(exps, i, 2, 1), (exps, i, 3, 1)]
            if q == 6 and i < FIRST_HELD:
                return [(park, i)]
            return []

        def spread(a, b):
            o = []
            done = 0
            for n, f in enumerate(a):
                o.append(f)
                want = (n + 1) * len(b) // len(a)
                while done < want:
                    o.append(b[done])
                    done += 1
            return o + list(b[done:])

        def run(fs):
            for f in fs:
                f[0](*f[1:])

        start = {}
        for i in range(NT):
            start[i] = KG + 2 + 2 * i
        last = start[NT - 1] + 2

        def w2_inter(g):
            interleave(nc.vector.tensor_copy, w2i[g][:], w2p[g][:])

        for tau in range(last + 1):
            live = []
            for i in range(NT):
                for q in (2 * (tau - start[i]), 2 * (tau - start[i]) + 1):
                    if 0 <= q <= 6:
                        live.append((i, q))
            begins = tau in start.values()
            v1 = []
            if 0 <= tau - 2 < NH:
                v1.append((flips, tau - 2))
            if 0 <= tau - 3 < NH:
                if begins:
                    quant(tau - 3)
                else:
                    v1.append((quant, tau - 3))
            for i, q in live:
                if q == 0:
                    logits(i)
            if tau < NH:
                mm(tau)
            u = (tau + 1) // 2
            fresh = tau % 2 == 1 and u < NCH * K
            if tau == 0:
                v1.append((w1_quant, 1))
            if fresh:
                v1.append((xr_mul, u))
            on_act = tau - 2 in ON_ACT
            if 0 <= tau - 2 < NH and not on_act:
                v1.append((inter, tau - 2, nc.vector.tensor_copy))
            if fresh:
                v1.append((xr_quant, u))
            if tau in (5, 8):
                v1.append((w2_inter, (tau - 5) // 3))
            if tau in (6, 9):
                v1.append((w2_quant, (tau - 6) // 3))
            v2 = []
            for i, q in live:
                v2 += s2_vec(i, q)
            a1 = []
            if 0 <= tau - 1 < NH:
                relu(tau - 1)
            run(spread(v2, v1) if v2 else v1)
            a2 = []
            for i, q in live:
                a2 += s2_act(i, q)
            if 0 <= tau - 2 < NH and on_act:
                a1.append((inter, tau - 2, nc.scalar.copy))
            run(spread(a2, a1) if a2 else a1)
            for i, q in live:
                if q == 3:
                    weights(i)
                    diag(i)
                    mix(i, 0)
                    mix(i, 1)
                if q == 4:
                    mix(i, 2)
                    mix(i, 3)
            if tau == 3:
                turn_x(2, nc.scalar.copy)
            if tau < 8:
                w2_widen(tau // 4, tau % 4)

        factor = keep.tile([P, 1], F32, name="factor")
        nc.vector.tensor_scalar(out=factor[:], in0=st[NT - 1]["d"][:, K - 1, C - 1:C], scalar1=0.0, scalar2=float(C) / K, op0=ALU.mult, op1=ALU.add)
        for i in range(NT):
            src = psb[:, i, :] if i < FIRST_HELD else st[i]["p"][:]
            nc.scalar.activation(out=psb[:, i, :], in_=src, func=ACT.Ln, scale=factor[:])
            o = keep.tile([P, C], F32, name="o%d" % i, align_bytes=64)
            nc.vector.tensor_tensor(out=o[:], in0=psb[:, i, :], in1=tn[i][:], op=ALU.subtract)
            nc.sync.dma_start(out=ov[:, i, :], in_=o[:])
